import numpy as np, ml_dtypes
CORES = [10,34,74,98]
N = 4
GR, GC = 2, 2
L, KA, KB, F = 4, 2, 2, 256
def setup_inputs(rng):
    return {"a": rng.standard_normal((N, 128, KA * 128), dtype=np.float32).astype(ml_dtypes.bfloat16), "b": rng.standard_normal((N, 128, KB * F), dtype=np.float32).astype(ml_dtypes.bfloat16)}
def setup_inputs_big(rng):
    d = setup_inputs(rng)
    for k in ("a", "b"): d[k] = (d[k].astype(np.float32) * 1024.0).astype(d[k].dtype)
    return d
def setup_inputs_small(rng):
    d = setup_inputs(rng)
    for k in ("a", "b"): d[k] = (d[k].astype(np.float32) * (1 / 1024.0)).astype(d[k].dtype)
    return d
def setup_inputs_apart(rng):
    d = setup_inputs(rng)
    f = (10.0 ** rng.permutation(np.linspace(-1.5, 1.5, N))).astype(np.float32).reshape(N, 1, 1)
    for k in ("a", "b"): d[k] = (d[k].astype(np.float32) * f).astype(d[k].dtype)
    return d
def reference(a, b):
    A, B = a.astype(np.float64), b.astype(np.float64)
    y = np.zeros((N, 128, F))
    for i in range(GR):
        for j in range(GC):
            for k in range(L):
                At = A[i * GC + k // KA][:, 128 * (k % KA):128 * (k % KA) + 128]
                Bt = B[(k // KB) * GC + j][:, F * (k % KB):F * (k % KB) + F]
                y[i * GC + j] += At.T @ Bt
    return {"y": y.astype(ml_dtypes.bfloat16 if a.dtype != np.float64 else np.float64)}

@@ -1,0 +1,78 @@
+GR, GC = 2, 2
+L, KA, KB, F = 4, 2, 2, 256
+
+SCRATCH = {
+    "a_sb": ("sbuf", [128, KA * 128], "bfloat16"),
+    "b_sb": ("sbuf", [128, KB * F], "bfloat16"),
+    "ra": ("sbuf", [128, KA * 128], "bfloat16"),
+    "rb": ("sbuf", [128, KB * F], "bfloat16"),
+    "acc": ("psum", [128, F], "float32"),
+    "y_sb": ("sbuf", [128, F], "bfloat16"),
+}
+SEMAPHORES = ["la", "lb", "arr_a", "arr_b", "sent", "mm", "cp", "st"]
+
+
+def _engines(mask):
+    return bin(mask).count("1")
+
+
+def rank_program(g, core, T, topo):
+    rank = T.rank_of(core)
+    if rank is None:
+        return
+    S = T.sem
+    row, col = rank // GC, rank % GC
+    row_peer = T.cores[row * GC + (1 - col)]
+    col_peer = T.cores[(1 - row) * GC + col]
+
+    g.scalar.dma_start(T.a_sb[:], T.a[:]).then_inc(S.la, 16)
+    g.sync.dma_start(T.b_sb[:], T.b[:]).then_inc(S.lb, 16)
+
+    left = 0
+    for peer, loaded, src, dst, arr in ((row_peer, S.la, T.a_sb, T.ra, S.arr_a),
+                                        (col_peer, S.lb, T.b_sb, T.rb, S.arr_b)):
+        if not topo.may_write(core, peer):
+            raise ValueError("core %d may not write to core %d" % (core, peer))
+        rid, pid, _ = topo.addr(peer)
+        m = topo.mask(core, peer)
+        g.wait_ge(loaded, 16)
+        g.remote_dma(out_ap=dst[:], in_ap=src[:], remote_sem=arr, local_sem=S.sent,
+                     pid=pid, routing_id=rid, dma_engine_mask=m)
+        left += _engines(m)
+    n_a = _engines(topo.mask(row_peer, core))
+    n_b = _engines(topo.mask(col_peer, core))
+
+    def key(k):
+        return (0 if k // KA == col else 1) + (0 if k // KB == row else 2)
+    order = sorted(range(L), key=key)
+    waited = set()
+
+    def need(sem, name, n):
+        if name not in waited:
+            waited.add(name)
+            g.tensor.wait_ge(sem, n)
+    for n, k in enumerate(order):
+        if k // KA == col:
+            need(S.la, "la", 16)
+            at = T.a_sb
+        else:
+            need(S.arr_a, "arr_a", n_a)
+            at = T.ra
+        if k // KB == row:
+            need(S.lb, "lb", 16)
+            bt = T.b_sb
+        else:
+            need(S.arr_b, "arr_b", n_b)
+            bt = T.rb
+        ta, tb = k % KA, k % KB
+        mmi = g.tensor.matmul(T.acc[:], at[:, 128 * ta:128 * ta + 128], bt[:, F * tb:F * tb + F],
+                              n == 0, n == L - 1)
+    mmi.then_inc(S.mm, 1)
+
+    g.vector.wait_ge(S.mm, 1)
+    g.vector.tensor_copy(T.y_sb[:], T.acc[:]).then_inc(S.cp, 1)
+    g.sync.wait_ge(S.cp, 1)
+    g.sync.dma_start(T.y[:], T.y_sb[:]).then_inc(S.st, 16)
+    g.sync.wait_ge(S.st, 16)
+
+    g.wait_ge(S.sent, left)

@@ -1,15 +1,19 @@
 GR, GC = 2, 2
 L, KA, KB, F = 4, 2, 2, 256
+H = F // 2
 
 SCRATCH = {
+    "a_dr": ("dram", [128, KA * 128], "bfloat16"),
     "a_sb": ("sbuf", [128, KA * 128], "bfloat16"),
-    "b_sb": ("sbuf", [128, KB * F], "bfloat16"),
+    "bw": ("sbuf", [128, 6 * H], "bfloat16"),
     "ra": ("sbuf", [128, KA * 128], "bfloat16"),
-    "rb": ("sbuf", [128, KB * F], "bfloat16"),
-    "acc": ("psum", [128, F], "float32"),
+    "rb": ("sbuf", [128, 4 * H], "bfloat16"),
+    "acc0": ("psum", [128, 512], "float32"),
+    "acc1": ("psum", [128, 512], "float32"),
     "y_sb": ("sbuf", [128, F], "bfloat16"),
 }
-SEMAPHORES = ["la", "lb", "arr_a", "arr_b", "sent", "mm", "cp", "st"]
+SEMAPHORES = ["ld", "la", "lb", "p0", "p1", "arr_a", "arr_h0", "arr_h1", "sent",
+              "mm0", "mm1", "cp0", "cp1", "st0", "st1"]
 
 
 def _engines(mask):
@@ -25,54 +29,69 @@ def rank_program(g, core, T, topo):
     row_peer = T.cores[row * GC + (1 - col)]
     col_peer = T.cores[(1 - row) * GC + col]
 
-    g.scalar.dma_start(T.a_sb[:], T.a[:]).then_inc(S.la, 16)
-    g.sync.dma_start(T.b_sb[:], T.b[:]).then_inc(S.lb, 16)
+    g.sync.dma_start(T.a_dr[:], T.a[:]).then_inc(S.ld, 16)
+    g.scalar.dma_start(T.bw[:, H:5 * H], T.b[:]).then_inc(S.lb, 16)
+    g.sync.dma_start(T.a_sb[:], T.a[:]).then_inc(S.la, 16)
+
+    g.vector.wait_ge(S.lb, 16)
+    g.vector.tensor_copy(T.bw[:, 0:H], T.bw[:, 3 * H:4 * H]).then_inc(S.p0, 1)
+    g.vector.tensor_copy(T.bw[:, 5 * H:6 * H], T.bw[:, 2 * H:3 * H]).then_inc(S.p1, 1)
 
     left = 0
-    for peer, loaded, src, dst, arr in ((row_peer, S.la, T.a_sb, T.ra, S.arr_a),
-                                        (col_peer, S.lb, T.b_sb, T.rb, S.arr_b)):
+    for peer, waits, src, dst, arr in (
+            (row_peer, ((S.ld, 16),), T.a_dr[:], T.ra[:], S.arr_a),
+            (col_peer, ((S.lb, 16), (S.p0, 1)), T.bw[:, 0:2 * H], T.rb[:, 0:2 * H], S.arr_h0),
+            (col_peer, ((S.p1, 1),), T.bw[:, 4 * H:6 * H], T.rb[:, 2 * H:4 * H], S.arr_h1)):
         if not topo.may_write(core, peer):
             raise ValueError("core %d may not write to core %d" % (core, peer))
         rid, pid, _ = topo.addr(peer)
         m = topo.mask(core, peer)
-        g.wait_ge(loaded, 16)
-        g.remote_dma(out_ap=dst[:], in_ap=src[:], remote_sem=arr, local_sem=S.sent,
+        for sem, n in waits:
+            g.wait_ge(sem, n)
+        g.remote_dma(out_ap=dst, in_ap=src, remote_sem=arr, local_sem=S.sent,
                      pid=pid, routing_id=rid, dma_engine_mask=m)
         left += _engines(m)
     n_a = _engines(topo.mask(row_peer, core))
     n_b = _engines(topo.mask(col_peer, core))
 
-    def key(k):
-        return (0 if k // KA == col else 1) + (0 if k // KB == row else 2)
-    order = sorted(range(L), key=key)
+    def stage(hk):
+        h, k = hk
+        if k // KB != row:
+            return 2 + h
+        return 0 if k // KA == col else 1
+    jobs = sorted([(h, k) for h in range(2) for k in range(L)], key=stage)
     waited = set()
 
-    def need(sem, name, n):
+    def need(name, n):
         if name not in waited:
             waited.add(name)
-            g.tensor.wait_ge(sem, n)
-    for n, k in enumerate(order):
+            g.tensor.wait_ge(S[name], n)
+    done = [0, 0]
+    for h, k in jobs:
+        ta, tb = k % KA, k % KB
         if k // KA == col:
-            need(S.la, "la", 16)
+            need("la", 16)
             at = T.a_sb
         else:
-            need(S.arr_a, "arr_a", n_a)
+            need("arr_a", n_a)
             at = T.ra
         if k // KB == row:
-            need(S.lb, "lb", 16)
-            bt = T.b_sb
+            need("lb", 16)
+            bt = T.bw[:, (1 + 2 * tb + h) * H:(2 + 2 * tb + h) * H]
         else:
-            need(S.arr_b, "arr_b", n_b)
-            bt = T.rb
-        ta, tb = k % KA, k % KB
-        mmi = g.tensor.matmul(T.acc[:], at[:, 128 * ta:128 * ta + 128], bt[:, F * tb:F * tb + F],
-                              n == 0, n == L - 1)
-    mmi.then_inc(S.mm, 1)
+            need("arr_h%d" % h, n_b)
+            bt = T.rb[:, (2 * h + 1 - tb) * H:(2 * h + 2 - tb) * H]
+        done[h] += 1
+        mmi = g.tensor.matmul(T["acc%d" % h][:, 0:H], at[:, 128 * ta:128 * ta + 128], bt,
+                              done[h] == 1, done[h] == L)
+        if done[h] == L:
+            mmi.then_inc(S["mm%d" % h], 1)
 
-    g.vector.wait_ge(S.mm, 1)
-    g.vector.tensor_copy(T.y_sb[:], T.acc[:]).then_inc(S.cp, 1)
-    g.sync.wait_ge(S.cp, 1)
-    g.sync.dma_start(T.y[:], T.y_sb[:]).then_inc(S.st, 16)
-    g.sync.wait_ge(S.st, 16)
+    for h, q in ((0, g.sync), (1, g.scalar)):
+        g.vector.wait_ge(S["mm%d" % h], 1)
+        g.vector.tensor_copy(T.y_sb[:, h * H:(h + 1) * H], T["acc%d" % h][:, 0:H]).then_inc(S["cp%d" % h], 1)
+        q.wait_ge(S["cp%d" % h], 1)
+        q.dma_start(T.y[:, h * H:(h + 1) * H], T.y_sb[:, h * H:(h + 1) * H]).then_inc(S["st%d" % h], 16)
+        q.wait_ge(S["st%d" % h], 16)
 
     g.wait_ge(S.sent, left)

GR, GC = 2, 2
L, KA, KB, F = 4, 2, 2, 256
H = F // 2

SCRATCH = {
    "a_dr": ("dram", [128, KA * 128], "bfloat16"),
    "a_sb": ("sbuf", [128, KA * 128], "bfloat16"),
    "bw": ("sbuf", [128, 6 * H], "bfloat16"),
    "ra": ("sbuf", [128, KA * 128], "bfloat16"),
    "rb": ("sbuf", [128, 4 * H], "bfloat16"),
    "acc0": ("psum", [128, 512], "float32"),
    "acc1": ("psum", [128, 512], "float32"),
    "y_sb": ("sbuf", [128, F], "bfloat16"),
}
SEMAPHORES = ["ld", "la", "lb", "p0", "p1", "arr_a", "arr_h0", "arr_h1", "sent",
              "mm0", "mm1", "cp0", "cp1", "st0", "st1"]


def _engines(mask):
    return bin(mask).count("1")


def rank_program(g, core, T, topo):
    rank = T.rank_of(core)
    if rank is None:
        return
    S = T.sem
    row, col = rank // GC, rank % GC
    row_peer = T.cores[row * GC + (1 - col)]
    col_peer = T.cores[(1 - row) * GC + col]

    g.sync.dma_start(T.a_dr[:], T.a[:]).then_inc(S.ld, 16)
    g.scalar.dma_start(T.bw[:, H:5 * H], T.b[:]).then_inc(S.lb, 16)
    g.sync.dma_start(T.a_sb[:], T.a[:]).then_inc(S.la, 16)

    g.vector.wait_ge(S.lb, 16)
    g.vector.tensor_copy(T.bw[:, 0:H], T.bw[:, 3 * H:4 * H]).then_inc(S.p0, 1)
    g.vector.tensor_copy(T.bw[:, 5 * H:6 * H], T.bw[:, 2 * H:3 * H]).then_inc(S.p1, 1)

    left = 0
    for peer, waits, src, dst, arr in (
            (row_peer, ((S.ld, 16),), T.a_dr[:], T.ra[:], S.arr_a),
            (col_peer, ((S.lb, 16), (S.p0, 1)), T.bw[:, 0:2 * H], T.rb[:, 0:2 * H], S.arr_h0),
            (col_peer, ((S.p1, 1),), T.bw[:, 4 * H:6 * H], T.rb[:, 2 * H:4 * H], S.arr_h1)):
        if not topo.may_write(core, peer):
            raise ValueError("core %d may not write to core %d" % (core, peer))
        rid, pid, _ = topo.addr(peer)
        m = topo.mask(core, peer)
        for sem, n in waits:
            g.wait_ge(sem, n)
        g.remote_dma(out_ap=dst, in_ap=src, remote_sem=arr, local_sem=S.sent,
                     pid=pid, routing_id=rid, dma_engine_mask=m)
        left += _engines(m)
    n_a = _engines(topo.mask(row_peer, core))
    n_b = _engines(topo.mask(col_peer, core))

    def stage(hk):
        h, k = hk
        if k // KB != row:
            return 2 + h
        return 0 if k // KA == col else 1
    jobs = sorted([(h, k) for h in range(2) for k in range(L)], key=stage)
    waited = set()

    def need(name, n):
        if name not in waited:
            waited.add(name)
            g.tensor.wait_ge(S[name], n)
    done = [0, 0]
    for h, k in jobs:
        ta, tb = k % KA, k % KB
        if k // KA == col:
            need("la", 16)
            at = T.a_sb
        else:
            need("arr_a", n_a)
            at = T.ra
        if k // KB == row:
            need("lb", 16)
            bt = T.bw[:, (1 + 2 * tb + h) * H:(2 + 2 * tb + h) * H]
        else:
            need("arr_h%d" % h, n_b)
            bt = T.rb[:, (2 * h + 1 - tb) * H:(2 * h + 2 - tb) * H]
        done[h] += 1
        mmi = g.tensor.matmul(T["acc%d" % h][:, 0:H], at[:, 128 * ta:128 * ta + 128], bt,
                              done[h] == 1, done[h] == L)
        if done[h] == L:
            mmi.then_inc(S["mm%d" % h], 1)

    for h, q in ((0, g.sync), (1, g.scalar)):
        g.vector.wait_ge(S["mm%d" % h], 1)
        g.vector.tensor_copy(T.y_sb[:, h * H:(h + 1) * H], T["acc%d" % h][:, 0:H]).then_inc(S["cp%d" % h], 1)
        q.wait_ge(S["cp%d" % h], 1)
        q.dma_start(T.y[:, h * H:(h + 1) * H], T.y_sb[:, h * H:(h + 1) * H]).then_inc(S["st%d" % h], 16)
        q.wait_ge(S["st%d" % h], 16)

    g.wait_ge(S.sent, left)
